import numpy as np
import ml_dtypes


def mxq(x, axis, fmt="e4m3"):
    dtype, down = {"e4m3": (ml_dtypes.float8_e4m3fn, 7), "e5m2": (ml_dtypes.float8_e5m2, 14)}[fmt]
    v = np.moveaxis(np.asarray(x, np.float32).astype(ml_dtypes.bfloat16).astype(np.float64), axis, -1)
    blocks = v.reshape(v.shape[:-1] + (-1, 32))
    amax = np.abs(blocks).max(-1, keepdims=True)
    byte = np.maximum(np.where(amax > 0, np.frexp(amax)[1] - 1 + 127, 0) - down, 1)
    scale = np.exp2(byte - 127.0)
    codes = (blocks / scale).astype(np.float32).astype(dtype).astype(np.float64)
    return np.moveaxis((codes * scale).reshape(v.shape), -1, axis)


WIDE = False


def mx_kscale(k):
    if not WIDE:
        return np.ones(k)
    levels = np.array([10, -10, 5, -5, 0])
    if k % 512:
        return np.exp2(np.random.permutation(np.resize(levels, k // 32))).repeat(32)
    a = np.empty((k // 512, 16))
    for p in range(k // 512):
        a[p, :8] = np.random.permutation(np.resize(levels, 8))
        for g in range(8):
            far = levels[np.abs(levels - a[p, g]) >= 10]
            a[p, g + 8] = far[np.random.randint(len(far))]
    return np.exp2(a.ravel()).repeat(32)


def f64(x):
    return np.asarray(x).astype(np.float64)


def striped(idx):
    return np.tile(idx.reshape(-1, 16).T, (8, 1)).astype(np.uint16)


def unstriped(offs):
    return offs[:16].T.reshape(-1).astype(np.int64)


E2M1 = np.array([0.0, 0.5, 1.0, 1.5, 2.0, 3.0, 4.0, 6.0, -0.0, -0.5, -1.0, -1.5, -2.0, -3.0, -4.0, -6.0])


def pack_weight(w, fmt):
    k, n = w.shape
    w = f64(np.asarray(w, np.float32).astype(ml_dtypes.bfloat16)).reshape(k // 32, 32, n)
    amax = np.abs(w).max(1)
    if fmt == "e4m3":
        byte = np.frexp(amax)[1] - 1 + 127 - 7
    else:
        mant, ex = np.frexp(amax / 6.0)
        byte = np.where(mant > 0.5, ex, ex - 1) + 127
    byte = np.clip(np.where(amax > 0, byte, 1), 1, 254)
    scaled = (w * np.exp2(127.0 - byte)[:, None, :]).reshape(k, n).astype(np.float32)
    by_word = np.ascontiguousarray(scaled.reshape(k // 512, 128, 4, n).transpose(0, 1, 3, 2))
    if fmt == "e4m3":
        words = by_word.astype(ml_dtypes.float8_e4m3fn).view(np.uint8)
    else:
        c = by_word.astype(ml_dtypes.float4_e2m1fn).view(np.uint8) & 0xF
        words = (c[..., 0::2] | (c[..., 1::2] << 4)).reshape(k // 512, 128, 2 * n)
    return np.ascontiguousarray(words), np.ascontiguousarray(byte.astype(np.uint8).reshape(k // 512, 16, n))


def unpack_weight(words, scales, fmt):
    g, _, n = scales.shape
    words = np.ascontiguousarray(words).reshape(g, 128, n, -1)
    if fmt == "e4m3":
        vals = words.view(ml_dtypes.float8_e4m3fn).astype(np.float64)
    else:
        nib = np.empty((g, 128, n, 4), np.uint8)
        nib[..., 0::2] = words & 0xF
        nib[..., 1::2] = words >> 4
        vals = E2M1[nib]
    vals = vals * np.repeat(np.exp2(scales.astype(np.float64) - 127.0), 8, axis=1)[..., None]
    return vals.transpose(0, 1, 3, 2).reshape(g * 512, n)


def gelu(v):
    return 0.5 * v * (1.0 + np.tanh(np.sqrt(2.0 / np.pi) * (v + 0.044715 * v**3)))


K, T, S, K2, H, N = 1024, 4096, 1024, 512, 1024, 512

def setup_inputs():
    n = np.random.standard_normal
    s = mx_kscale(K)[:, None]
    s2 = mx_kscale(K2)[:, None]
    u = mx_kscale(H)[:, None]
    d = {}
    d["tab_words"], d["tab_scales"] = pack_weight(n((K, T)) * s, "e4m3")
    d["offs"] = striped(np.random.permutation(T)[:S])
    d["xs_words"], d["xs_scales"] = pack_weight(n((K2, S)) * s2, "e4m3")
    d["w1"] = (n((K, H)) / K ** 0.5 / s * u.T).astype(np.float32)
    d["w2_words"], d["w2_scales"] = pack_weight(n((K2, H)) / K2 ** 0.5 / s2 * u.T, "e2m1")
    d["w3"] = (n((H, N)) / H ** 0.5 / u).astype(np.float32)
    d["bias"] = (0.6 * n(N)).astype(np.float32)
    return d

def reference(tab_words, tab_scales, offs, xs_words, xs_scales, w1, w2_words, w2_scales, w3, bias):
    v = unpack_weight(tab_words, tab_scales, "e4m3")[:, unstriped(offs)]
    xs = unpack_weight(xs_words, xs_scales, "e4m3")
    w2 = unpack_weight(w2_words, w2_scales, "e2m1")
    ground = mxq(f64(w1), 0, "e4m3").T @ v
    cutter = w2.T @ xs
    h = np.maximum(ground, cutter)
    y = mxq(f64(w3), 0, "e4m3").T @ mxq(h, 0, "e4m3")
    return y + f64(bias)[:, None]

@@ -1,0 +1,246 @@
+from contextlib import ExitStack
+
+import concourse.mybir as mybir
+
+K, T, S, K2, H, N = 1024, 4096, 1024, 512, 1024, 512
+FLOPS = 2 * S * (K * H + K2 * H + H * N)
+
+F32 = mybir.dt.float32
+BF16 = mybir.dt.bfloat16
+I32 = mybir.dt.int32
+U32 = mybir.dt.uint32
+U16 = mybir.dt.uint16
+U8 = mybir.dt.uint8
+FP8X4 = mybir.dt.float8_e4m3fn_x4
+FP4X4 = mybir.dt.float4_e2m1fn_x4
+ALU = mybir.AluOpType
+ACT = mybir.ActivationFunctionType
+
+P = 128
+PACK = 4
+KP = P * PACK
+JC = 128
+GW = 256
+
+
+def tile_list_ground_sensor_larger_kernel(
+    tc, tab_words, tab_scales, offs, xs_words, xs_scales, w1, w2_words, w2_scales, w3, bias, out
+):
+    nc = tc.nc
+    with ExitStack() as ctx:
+        keep = ctx.enter_context(tc.tile_pool(name="keep", bufs=1))
+        psum = ctx.enter_context(tc.psum_pool(name="psum", bufs=8))
+
+        def tile(name, shape, dtype):
+            return keep.tile(shape, dtype, name=name, align_bytes=64)
+
+        offsets = keep.tile([P, S // 16], U16, name="offsets")
+        w2_sc_raw = tile("w2_sc_raw", [P, H], U8)
+        xs_sc = tile("xs_sc", [P, S], U8)
+        tab_sc = tile("tab_sc", [P, T], U8)
+        nc.gpsimd.memset(w2_sc_raw[:].bitcast(I32), 0)
+        nc.gpsimd.memset(xs_sc[:].bitcast(I32), 0)
+        nc.vector.memset(tab_sc[:].bitcast(I32), 0)
+
+        w2_raw = tile("w2_raw", [P, 2 * H], U8)
+        xs = tile("xs", [P, S], U32)
+        nc.sync.dma_start(out=w2_raw[:].bitcast(I32), in_=w2_words[0].bitcast(I32))
+        nc.sync.dma_start(out=xs[:].bitcast(I32), in_=xs_words[0].rearrange("p c i -> p (c i)").bitcast(I32))
+        for q in range(4):
+            nc.sync.dma_start(
+                out=w2_sc_raw[32 * q : 32 * q + 4, :].bitcast(I32), in_=w2_scales[0, 4 * q : 4 * q + 4, :].bitcast(I32)
+            )
+
+        def load_xs_scales(q):
+            nc.sync.dma_start(
+                out=xs_sc[32 * q : 32 * q + 4, :].bitcast(I32), in_=xs_scales[0, 4 * q : 4 * q + 4, :].bitcast(I32)
+            )
+
+        def load_weight(name, rows):
+            raw = tile(name, [P, PACK, KP], F32)
+            nc.sync.dma_start(out=raw[:], in_=rows.rearrange("(p j) c -> p j c", j=PACK))
+            return raw
+
+        def load_table(a):
+            words = tile(f"tab{a}", [P, T], U32)
+            nc.sync.dma_start(out=words[:].bitcast(I32), in_=tab_words[a].rearrange("p t i -> p (t i)").bitcast(I32))
+            return words
+
+        w1_raw = {}
+        tab = {}
+        load_xs_scales(0)
+        w1_raw[0, 0] = load_weight("w1_raw00", w1[0:KP, 0:KP])
+        for q in range(1, 4):
+            load_xs_scales(q)
+        tab[0] = load_table(0)
+        for q in range(4):
+            nc.sync.dma_start(
+                out=tab_sc[32 * q : 32 * q + 8, :].bitcast(I32), in_=tab_scales[:, 4 * q : 4 * q + 4, :].bitcast(I32)
+            )
+        nc.sync.dma_start(offsets[:], offs)
+        w1_raw[0, 1] = load_weight("w1_raw01", w1[KP:K, 0:KP])
+        tab[1] = load_table(1)
+        bias_sb = tile("bias_sb", [P, PACK], F32)
+        nc.sync.dma_start(out=bias_sb[:], in_=bias.rearrange("(p q) -> p q", q=PACK))
+        w1_raw[1, 0] = load_weight("w1_raw10", w1[0:KP, KP:H])
+        w1_raw[1, 1] = load_weight("w1_raw11", w1[KP:K, KP:H])
+        w3_raw = [load_weight(f"w3_raw{b}", w3[b * KP : (b + 1) * KP, :]) for b in range(2)]
+
+        w2c = tile("w2c", [P, 2 * H], U8)
+        w2s = tile("w2s", [P, H], U8)
+        for b in range(2):
+            nc.vector.tensor_copy(
+                out=w2c[:, b * 2 * KP : (b + 1) * 2 * KP].rearrange("p (t m e) -> p m t e", t=PACK, e=2),
+                in_=w2_raw[:, b * 2 * KP : (b + 1) * 2 * KP].rearrange("p (m t e) -> p m t e", t=PACK, e=2),
+            )
+            nc.vector.tensor_copy(
+                out=w2s[:, b * KP : (b + 1) * KP].rearrange("p (t m) -> p m t", t=PACK),
+                in_=w2_sc_raw[:, b * KP : (b + 1) * KP].rearrange("p (m t) -> p m t", t=PACK),
+            )
+
+        cutter = {}
+        for b in range(2):
+            for jc in range(S // JC):
+                cols = slice(jc * JC, (jc + 1) * JC)
+                bank = psum.tile([P, PACK, JC], F32, name="bank")
+                for t in range(PACK):
+                    c0 = b * KP + t * P
+                    nc.tensor.matmul_mx(
+                        out=bank[:, t, :],
+                        lhsT=w2c[:, 2 * c0 : 2 * (c0 + P)].bitcast(FP4X4),
+                        lhsT_scale=w2s[:, c0 : c0 + P],
+                        rhs=xs[:, cols].bitcast(FP8X4),
+                        rhs_scale=xs_sc[:, cols],
+                        start=True,
+                        stop=True,
+                    )
+                cutter[b, jc] = tile(f"cutter{b}_{jc}", [P, JC, PACK], F32)
+                nc.scalar.copy(out=cutter[b, jc][:], in_=bank[:].rearrange("p t j -> p j t"))
+
+        def round_weight(copy, name, raw):
+            grouped = tile(name, [P, KP * PACK], BF16)
+            copy(
+                out=grouped[:].rearrange("p (t m j) -> p m j t", t=PACK, j=PACK),
+                in_=raw[:].rearrange("p j (m t) -> p m j t", t=PACK),
+            )
+            return grouped
+
+        def quantize(name, grouped):
+            width = grouped.shape[1] // PACK
+            codes = tile(name + "_codes", [P, width], U32)
+            scales = tile(name + "_scales", [P, width], U8)
+            nc.vector.quantize_mx(out=codes[:].bitcast(FP8X4), scales=scales[:], in_=grouped)
+            return codes, scales
+
+        def gather(name, window, dtype, j0, width):
+            picked = tile(name, [P, width], dtype)
+            nc.vector.tensor_copy(picked[:], window[:].indirect(offsets[:, j0 // 16 : (j0 + width) // 16]))
+            return picked
+
+        w1q = {}
+        w1_bf = {}
+        w1_bf[0, 0] = round_weight(nc.vector.tensor_copy, "w1_bf00", w1_raw[0, 0])
+        v_sc = gather("v_sc", tab_sc, U8, 0, S)
+        w1q[0, 0] = quantize("w1q00", w1_bf[0, 0][:])
+        v = {}
+        v[0] = gather("v0", tab[0], U32, 0, S)
+        w1_bf[0, 1] = round_weight(nc.vector.tensor_copy, "w1_bf01", w1_raw[0, 1])
+        w1q[0, 1] = quantize("w1q01", w1_bf[0, 1][:])
+        for a in range(2):
+            w1_bf[1, a] = round_weight(nc.scalar.copy, f"w1_bf1{a}", w1_raw[1, a])
+        w3_bf = [round_weight(nc.scalar.copy, f"w3_bf{b}", w3_raw[b]) for b in range(2)]
+
+        v1 = {}
+
+        def v_cols(a, jc):
+            if a == 0:
+                return v[0][:, jc * JC : (jc + 1) * JC]
+            g, r = divmod(jc * JC, GW)
+            return v1[g][:, r : r + JC]
+
+        h_bf = {}
+
+        def larger(b, jc, dst):
+            cols = slice(jc * JC, (jc + 1) * JC)
+            bank = psum.tile([P, PACK, JC], F32, name="bank")
+            for a in range(2):
+                codes, scales = w1q[b, a]
+                for t in range(PACK):
+                    nc.tensor.matmul_mx(
+                        out=bank[:, t, :],
+                        lhsT=codes[:, t * P : (t + 1) * P].bitcast(FP8X4),
+                        lhsT_scale=scales[:, t * P : (t + 1) * P],
+                        rhs=v_cols(a, jc).bitcast(FP8X4),
+                        rhs_scale=v_sc[4 * a : P, cols],
+                        start=(a == 0 and t == 0),
+                        stop=(a == 1 and t == PACK - 1),
+                    )
+            nc.vector.tensor_tensor(
+                out=dst.rearrange("p (j t) -> p j t", t=PACK),
+                in0=bank[:].rearrange("p t j -> p j t"),
+                in1=cutter[b, jc][:],
+                op=ALU.max,
+            )
+
+        hq = {}
+
+        def h_chunk(b, j0, width):
+            h_bf[b, j0] = tile(f"h_bf{b}_{j0}", [P, width * PACK], BF16)
+            for i in range(width // JC):
+                jc = j0 // JC + i
+                if b == 0 and (jc * JC) % GW == 0:
+                    g = jc * JC // GW
+                    for gg in ([0, 1] if g == 0 else [g + 1] if (g + 1) * GW < S else []):
+                        v1[gg] = gather(f"v1_{gg}", tab[1], U32, gg * GW, GW)
+                larger(b, jc, h_bf[b, j0][:, i * JC * PACK : (i + 1) * JC * PACK])
+
+        def h_quant(b, j0):
+            hq[b, j0] = quantize(f"hq{b}_{j0}", h_bf[b, j0][:])
+
+        out_v = out.rearrange("(p q) j -> p q j", q=PACK)
+
+        def project(j0, width, per_bank, engines):
+            h0 = (j0 // 512) * 512
+            moving = [
+                (hq[0, h0][0][:, j0 - h0 : j0 - h0 + width], hq[0, h0][1][:, j0 - h0 : j0 - h0 + width]),
+                (hq[1, j0][0][:], hq[1, j0][1][:]),
+            ]
+            for q0 in range(0, PACK, per_bank):
+                bank = psum.tile([P, per_bank, width], F32, name="bank")
+                for b in range(2):
+                    for i in range(per_bank):
+                        q = q0 + i
+                        nc.tensor.matmul_mx(
+                            out=bank[:, i, :],
+                            lhsT=w3q[b][0][:, q * P : (q + 1) * P].bitcast(FP8X4),
+                            lhsT_scale=w3q[b][1][:, q * P : (q + 1) * P],
+                            rhs=moving[b][0].bitcast(FP8X4),
+                            rhs_scale=moving[b][1],
+                            start=(b == 0 and i == 0),
+                            stop=(b == 1 and i == per_bank - 1),
+                        )
+                y = tile(f"y{j0}_{q0}", [P, per_bank, width], F32)
+                for i in range(per_bank):
+                    col = bias_sb[:, q0 + i : q0 + i + 1]
+                    if engines[q0 // per_bank] == "scalar":
+                        nc.scalar.activation(out=y[:, i, :], in_=bank[:, i, :], func=ACT.Identity, bias=col)
+                    else:
+                        nc.vector.tensor_scalar(y[:, i, :], bank[:, i, :], col, None, ALU.add)
+                nc.sync.dma_start(out=out_v[:, q0 : q0 + per_bank, j0 : j0 + width], in_=y[:])
+
+        h_chunk(0, 0, 512)
+        h_chunk(0, 512, 512)
+        w1q[1, 0] = quantize("w1q10", w1_bf[1, 0][:])
+        w1q[1, 1] = quantize("w1q11", w1_bf[1, 1][:])
+        h_quant(0, 0)
+        h_quant(0, 512)
+        h_chunk(1, 0, 512)
+        w3q = [quantize(f"w3q{b}", w3_bf[b][:]) for b in range(2)]
+        h_quant(1, 0)
+        h_chunk(1, 512, 256)
+        project(0, 512, 1, ["scalar"] * 4)
+        h_chunk(1, 768, 256)
+        h_quant(1, 512)
+        project(512, 256, 2, ["scalar", "scalar"])
+        h_quant(1, 768)
+        project(768, 256, 2, ["vector", "scalar"])

@@ -46,57 +46,68 @@ def tile_list_ground_sensor_larger_kernel(
         xs = tile("xs", [P, S], U32)
         nc.sync.dma_start(out=w2_raw[:].bitcast(I32), in_=w2_words[0].bitcast(I32))
         nc.sync.dma_start(out=xs[:].bitcast(I32), in_=xs_words[0].rearrange("p c i -> p (c i)").bitcast(I32))
-        for q in range(4):
-            nc.sync.dma_start(
-                out=w2_sc_raw[32 * q : 32 * q + 4, :].bitcast(I32), in_=w2_scales[0, 4 * q : 4 * q + 4, :].bitcast(I32)
-            )
 
-        def load_xs_scales(q):
-            nc.sync.dma_start(
-                out=xs_sc[32 * q : 32 * q + 4, :].bitcast(I32), in_=xs_scales[0, 4 * q : 4 * q + 4, :].bitcast(I32)
-            )
+        def load_scale_row(plane, first, rows, r):
+            nc.sync.dma_start(out=plane[first + r : P : 32, :].bitcast(I32), in_=rows[r:16:4, :].bitcast(I32))
 
-        def load_weight(name, rows):
-            raw = tile(name, [P, PACK, KP], F32)
+        def load_w1(b, a):
+            raw = tile(f"w1_raw{b}{a}", [P, PACK, KP], F32)
+            rows = w1[a * KP : (a + 1) * KP, b * KP : (b + 1) * KP]
             nc.sync.dma_start(out=raw[:], in_=rows.rearrange("(p j) c -> p j c", j=PACK))
             return raw
 
-        def load_table(a):
-            words = tile(f"tab{a}", [P, T], U32)
-            nc.sync.dma_start(out=words[:].bitcast(I32), in_=tab_words[a].rearrange("p t i -> p (t i)").bitcast(I32))
-            return words
+        def load_w3(b):
+            raw = tile(f"w3_raw{b}", [P, PACK, N], F32)
+            rows = w3[b * KP : (b + 1) * KP, :].rearrange("(u t e) n -> t u e n", t=PACK, e=PACK)
+            for t in range(PACK):
+                nc.sync.dma_start(out=raw[:, t, :], in_=rows[t])
+            return raw
+
+        tab = [tile(f"tab{a}", [P, T], U32) for a in range(2)]
+
+        def load_table(a, half):
+            cols = slice(half * T // 2, (half + 1) * T // 2)
+            words = tab_words[a].rearrange("p t i -> p (t i)").bitcast(I32)
+            nc.sync.dma_start(out=tab[a][:, cols].bitcast(I32), in_=words[:, cols])
+
+        def load_tab_scale_row(i):
+            r, a = divmod(i, 2)
+            load_scale_row(tab_sc, 4 + 4 * a, tab_scales[a], r)
 
         w1_raw = {}
-        tab = {}
-        load_xs_scales(0)
-        w1_raw[0, 0] = load_weight("w1_raw00", w1[0:KP, 0:KP])
-        for q in range(1, 4):
-            load_xs_scales(q)
-        tab[0] = load_table(0)
-        for q in range(4):
-            nc.sync.dma_start(
-                out=tab_sc[32 * q : 32 * q + 8, :].bitcast(I32), in_=tab_scales[:, 4 * q : 4 * q + 4, :].bitcast(I32)
-            )
+        for r in range(4):
+            load_scale_row(w2_sc_raw, 0, w2_scales[0], r)
+        load_scale_row(xs_sc, 0, xs_scales[0], 0)
+        w1_raw[0, 0] = load_w1(0, 0)
+        for r in range(1, 4):
+            load_scale_row(xs_sc, 0, xs_scales[0], r)
+        load_table(0, 0)
+        for i in range(4):
+            load_tab_scale_row(i)
+        load_table(0, 1)
+        for i in range(4, 8):
+            load_tab_scale_row(i)
         nc.sync.dma_start(offsets[:], offs)
-        w1_raw[0, 1] = load_weight("w1_raw01", w1[KP:K, 0:KP])
-        tab[1] = load_table(1)
+        load_table(1, 0)
+        load_table(1, 1)
+        w1_raw[0, 1] = load_w1(0, 1)
+        w1_raw[1, 0] = load_w1(1, 0)
+        w1_raw[1, 1] = load_w1(1, 1)
         bias_sb = tile("bias_sb", [P, PACK], F32)
-        nc.sync.dma_start(out=bias_sb[:], in_=bias.rearrange("(p q) -> p q", q=PACK))
-        w1_raw[1, 0] = load_weight("w1_raw10", w1[0:KP, KP:H])
-        w1_raw[1, 1] = load_weight("w1_raw11", w1[KP:K, KP:H])
-        w3_raw = [load_weight(f"w3_raw{b}", w3[b * KP : (b + 1) * KP, :]) for b in range(2)]
+        with nc.allow_non_contiguous_dma(reason="one bias value a partition and output tile"):
+            nc.sync.dma_start(out=bias_sb[:], in_=bias.rearrange("(q p) -> p q", q=PACK))
+        w3_raw = [load_w3(b) for b in range(2)]
 
         w2c = tile("w2c", [P, 2 * H], U8)
         w2s = tile("w2s", [P, H], U8)
-        for b in range(2):
-            nc.vector.tensor_copy(
-                out=w2c[:, b * 2 * KP : (b + 1) * 2 * KP].rearrange("p (t m e) -> p m t e", t=PACK, e=2),
-                in_=w2_raw[:, b * 2 * KP : (b + 1) * 2 * KP].rearrange("p (m t e) -> p m t e", t=PACK, e=2),
-            )
-            nc.vector.tensor_copy(
-                out=w2s[:, b * KP : (b + 1) * KP].rearrange("p (t m) -> p m t", t=PACK),
-                in_=w2_sc_raw[:, b * KP : (b + 1) * KP].rearrange("p (m t) -> p m t", t=PACK),
-            )
+        nc.vector.tensor_copy(
+            out=w2c[:].bitcast(I32).rearrange("p (b t u w) -> p b t u w", b=2, t=PACK, w=2),
+            in_=w2_raw[:].bitcast(I32).rearrange("p (b u t w) -> p b t u w", b=2, t=PACK, w=2),
+        )
+        nc.vector.tensor_copy(
+            out=w2s[:].bitcast(I32).rearrange("p (b t u) -> p b t u", b=2, t=PACK),
+            in_=w2_sc_raw[:].bitcast(I32).rearrange("p (b u t) -> p b t u", b=2, t=PACK),
+        )
 
         cutter = {}
         for b in range(2):
@@ -120,8 +131,16 @@ def tile_list_ground_sensor_larger_kernel(
         def round_weight(copy, name, raw):
             grouped = tile(name, [P, KP * PACK], BF16)
             copy(
-                out=grouped[:].rearrange("p (t m j) -> p m j t", t=PACK, j=PACK),
-                in_=raw[:].rearrange("p j (m t) -> p m j t", t=PACK),
+                out=grouped[:].rearrange("p (t u e j) -> p t u j e", t=PACK, e=PACK, j=PACK),
+                in_=raw[:].rearrange("p j (u t e) -> p t u j e", t=PACK, e=PACK),
+            )
+            return grouped
+
+        def round_w3(copy, name, raw):
+            grouped = tile(name, [P, N * PACK], BF16)
+            copy(
+                out=grouped[:].rearrange("p (c e t) -> p c t e", e=PACK, t=PACK),
+                in_=raw[:].rearrange("p t (c e) -> p c t e", e=PACK),
             )
             return grouped
 
@@ -144,60 +163,63 @@ def tile_list_ground_sensor_larger_kernel(
         w1q[0, 0] = quantize("w1q00", w1_bf[0, 0][:])
         v = {}
         v[0] = gather("v0", tab[0], U32, 0, S)
-        w1_bf[0, 1] = round_weight(nc.vector.tensor_copy, "w1_bf01", w1_raw[0, 1])
-        w1q[0, 1] = quantize("w1q01", w1_bf[0, 1][:])
+        v[1] = gather("v1", tab[1], U32, 0, S)
+        w1_bf[0, 1] = tile("w1_bf01", [P, KP * PACK], BF16)
+        dealt = w1_bf[0, 1][:].rearrange("p (t u e j) -> p t u j e", t=PACK, e=PACK, j=PACK)
+        source = w1_raw[0, 1][:].rearrange("p j (u t e) -> p t u j e", t=PACK, e=PACK)
+        nc.vector.tensor_copy(out=dealt[:, 0:2], in_=source[:, 0:2])
+        nc.scalar.copy(out=dealt[:, 2:4], in_=source[:, 2:4])
+        w1q[0, 1] = (tile("w1q01_codes", [P, KP], U32), tile("w1q01_scales", [P, KP], U8))
+        for half in range(2):
+            cols = slice(half * KP // 2, (half + 1) * KP // 2)
+            nc.vector.quantize_mx(
+                out=w1q[0, 1][0][:, cols].bitcast(FP8X4),
+                scales=w1q[0, 1][1][:, cols],
+                in_=w1_bf[0, 1][:, half * 2 * KP : (half + 1) * 2 * KP],
+            )
         for a in range(2):
             w1_bf[1, a] = round_weight(nc.scalar.copy, f"w1_bf1{a}", w1_raw[1, a])
-        w3_bf = [round_weight(nc.scalar.copy, f"w3_bf{b}", w3_raw[b]) for b in range(2)]
+        w3_bf = [round_w3(nc.scalar.copy, f"w3_bf{b}", w3_raw[b]) for b in range(2)]
 
-        v1 = {}
+        banks = {}
 
-        def v_cols(a, jc):
-            if a == 0:
-                return v[0][:, jc * JC : (jc + 1) * JC]
-            g, r = divmod(jc * JC, GW)
-            return v1[g][:, r : r + JC]
-
-        h_bf = {}
-
-        def larger(b, jc, dst):
+        def ground(b, jc):
             cols = slice(jc * JC, (jc + 1) * JC)
-            bank = psum.tile([P, PACK, JC], F32, name="bank")
+            banks[b, jc] = psum.tile([P, PACK, JC], F32, name="bank")
             for a in range(2):
                 codes, scales = w1q[b, a]
                 for t in range(PACK):
                     nc.tensor.matmul_mx(
-                        out=bank[:, t, :],
+                        out=banks[b, jc][:, t, :],
                         lhsT=codes[:, t * P : (t + 1) * P].bitcast(FP8X4),
                         lhsT_scale=scales[:, t * P : (t + 1) * P],
-                        rhs=v_cols(a, jc).bitcast(FP8X4),
-                        rhs_scale=v_sc[4 * a : P, cols],
+                        rhs=v[a][:, cols].bitcast(FP8X4),
+                        rhs_scale=v_sc[4 + 4 * a : P, cols],
                         start=(a == 0 and t == 0),
                         stop=(a == 1 and t == PACK - 1),
                     )
+
+        widths = (512, 256)
+        h_bf = {
+            (b, j0): tile(f"h_bf{b}_{j0}", [P, widths[b] * PACK], BF16) for b in range(2) for j0 in range(0, S, widths[b])
+        }
+
+        def larger(b, jc):
+            j0 = jc * JC // widths[b] * widths[b]
+            c0 = (jc * JC - j0) * PACK
             nc.vector.tensor_tensor(
-                out=dst.rearrange("p (j t) -> p j t", t=PACK),
-                in0=bank[:].rearrange("p t j -> p j t"),
+                out=h_bf[b, j0][:, c0 : c0 + JC * PACK].rearrange("p (j t) -> p j t", t=PACK),
+                in0=banks[b, jc][:].rearrange("p t j -> p j t"),
                 in1=cutter[b, jc][:],
                 op=ALU.max,
             )
 
         hq = {}
 
-        def h_chunk(b, j0, width):
-            h_bf[b, j0] = tile(f"h_bf{b}_{j0}", [P, width * PACK], BF16)
-            for i in range(width // JC):
-                jc = j0 // JC + i
-                if b == 0 and (jc * JC) % GW == 0:
-                    g = jc * JC // GW
-                    for gg in ([0, 1] if g == 0 else [g + 1] if (g + 1) * GW < S else []):
-                        v1[gg] = gather(f"v1_{gg}", tab[1], U32, gg * GW, GW)
-                larger(b, jc, h_bf[b, j0][:, i * JC * PACK : (i + 1) * JC * PACK])
-
         def h_quant(b, j0):
             hq[b, j0] = quantize(f"hq{b}_{j0}", h_bf[b, j0][:])
 
-        out_v = out.rearrange("(p q) j -> p q j", q=PACK)
+        out_v = out.rearrange("(q p) j -> p q j", q=PACK)
 
         def project(j0, width, per_bank, engines):
             h0 = (j0 // 512) * 512
@@ -228,19 +250,36 @@ def tile_list_ground_sensor_larger_kernel(
                         nc.vector.tensor_scalar(y[:, i, :], bank[:, i, :], col, None, ALU.add)
                 nc.sync.dma_start(out=out_v[:, q0 : q0 + per_bank, j0 : j0 + width], in_=y[:])
 
-        h_chunk(0, 0, 512)
-        h_chunk(0, 512, 512)
-        w1q[1, 0] = quantize("w1q10", w1_bf[1, 0][:])
-        w1q[1, 1] = quantize("w1q11", w1_bf[1, 1][:])
-        h_quant(0, 0)
+        w3q = {}
+        for jc in range(8):
+            ground(0, jc)
+            larger(0, jc)
+            if jc == 3:
+                w1q[1, 0] = quantize("w1q10", w1_bf[1, 0][:])
+            if jc == 4:
+                h_quant(0, 0)
+            if jc == 5:
+                w1q[1, 1] = quantize("w1q11", w1_bf[1, 1][:])
+        for jc in range(6):
+            ground(1, jc)
+        larger(1, 0)
         h_quant(0, 512)
-        h_chunk(1, 0, 512)
-        w3q = [quantize(f"w3q{b}", w3_bf[b][:]) for b in range(2)]
+        w3q[0] = quantize("w3q0", w3_bf[0][:])
+        larger(1, 1)
+        w3q[1] = quantize("w3q1", w3_bf[1][:])
         h_quant(1, 0)
-        h_chunk(1, 512, 256)
-        project(0, 512, 1, ["scalar"] * 4)
-        h_chunk(1, 768, 256)
+        larger(1, 2)
+        project(0, 256, 2, ["scalar", "scalar"])
+        ground(1, 6)
+        ground(1, 7)
+        larger(1, 3)
+        larger(1, 4)
+        h_quant(1, 256)
+        project(256, 256, 2, ["scalar", "scalar"])
+        larger(1, 5)
+        larger(1, 6)
         h_quant(1, 512)
         project(512, 256, 2, ["scalar", "scalar"])
+        larger(1, 7)
         h_quant(1, 768)
         project(768, 256, 2, ["vector", "scalar"])

@@ -20,7 +20,7 @@ P = 128
 PACK = 4
 KP = P * PACK
 JC = 128
-GW = 256
+YW = 256
 
 
 def tile_list_ground_sensor_larger_kernel(
@@ -50,15 +50,15 @@ def tile_list_ground_sensor_larger_kernel(
         def load_scale_row(plane, first, rows, r):
             nc.sync.dma_start(out=plane[first + r : P : 32, :].bitcast(I32), in_=rows[r:16:4, :].bitcast(I32))
 
-        def load_w1(b, a):
-            raw = tile(f"w1_raw{b}{a}", [P, PACK, KP], F32)
-            rows = w1[a * KP : (a + 1) * KP, b * KP : (b + 1) * KP]
+        def load_w1(a, c0, width):
+            raw = tile(f"w1_raw{a}_{c0}", [P, PACK, width], F32)
+            rows = w1[a * KP : (a + 1) * KP, c0 : c0 + width]
             nc.sync.dma_start(out=raw[:], in_=rows.rearrange("(p j) c -> p j c", j=PACK))
             return raw
 
-        def load_w3(b):
-            raw = tile(f"w3_raw{b}", [P, PACK, N], F32)
-            rows = w3[b * KP : (b + 1) * KP, :].rearrange("(u t e) n -> t u e n", t=PACK, e=PACK)
+        def load_w3(b, n0, width):
+            raw = tile(f"w3_raw{b}_{n0}", [P, PACK, width], F32)
+            rows = w3[b * KP : (b + 1) * KP, n0 : n0 + width].rearrange("(u t e) n -> t u e n", t=PACK, e=PACK)
             for t in range(PACK):
                 nc.sync.dma_start(out=raw[:, t, :], in_=rows[t])
             return raw
@@ -78,7 +78,7 @@ def tile_list_ground_sensor_larger_kernel(
         for r in range(4):
             load_scale_row(w2_sc_raw, 0, w2_scales[0], r)
         load_scale_row(xs_sc, 0, xs_scales[0], 0)
-        w1_raw[0, 0] = load_w1(0, 0)
+        w1_raw[0, 0] = load_w1(0, 0, KP)
         for r in range(1, 4):
             load_scale_row(xs_sc, 0, xs_scales[0], r)
         load_table(0, 0)
@@ -90,13 +90,13 @@ def tile_list_ground_sensor_larger_kernel(
         nc.sync.dma_start(offsets[:], offs)
         load_table(1, 0)
         load_table(1, 1)
-        w1_raw[0, 1] = load_w1(0, 1)
-        w1_raw[1, 0] = load_w1(1, 0)
-        w1_raw[1, 1] = load_w1(1, 1)
+        w1_last = [load_w1(1, half * KP // 2, KP // 2) for half in range(2)]
+        w1_raw[1, 0] = load_w1(0, KP, KP)
+        w1_raw[1, 1] = load_w1(1, KP, KP)
+        w3_raw = [load_w3(0, 0, N), load_w3(1, 0, N // 2), load_w3(1, N // 2, N // 2)]
         bias_sb = tile("bias_sb", [P, PACK], F32)
         with nc.allow_non_contiguous_dma(reason="one bias value a partition and output tile"):
             nc.sync.dma_start(out=bias_sb[:], in_=bias.rearrange("(q p) -> p q", q=PACK))
-        w3_raw = [load_w3(b) for b in range(2)]
 
         w2c = tile("w2c", [P, 2 * H], U8)
         w2s = tile("w2s", [P, H], U8)
@@ -111,13 +111,14 @@ def tile_list_ground_sensor_larger_kernel(
 
         cutter = {}
         for b in range(2):
-            for jc in range(S // JC):
-                cols = slice(jc * JC, (jc + 1) * JC)
-                bank = psum.tile([P, PACK, JC], F32, name="bank")
+            for j0 in range(0, S, 512):
+                cols = slice(j0, j0 + 512)
+                cutter[b, j0] = tile(f"cutter{b}_{j0}", [P, PACK, 512], F32)
                 for t in range(PACK):
                     c0 = b * KP + t * P
+                    bank = psum.tile([P, 512], F32, name="bank")
                     nc.tensor.matmul_mx(
-                        out=bank[:, t, :],
+                        out=bank[:],
                         lhsT=w2c[:, 2 * c0 : 2 * (c0 + P)].bitcast(FP4X4),
                         lhsT_scale=w2s[:, c0 : c0 + P],
                         rhs=xs[:, cols].bitcast(FP8X4),
@@ -125,8 +126,8 @@ def tile_list_ground_sensor_larger_kernel(
                         start=True,
                         stop=True,
                     )
-                cutter[b, jc] = tile(f"cutter{b}_{jc}", [P, JC, PACK], F32)
-                nc.scalar.copy(out=cutter[b, jc][:], in_=bank[:].rearrange("p t j -> p j t"))
+                    copy = nc.vector.tensor_copy if b == 0 and t % 2 == 1 else nc.scalar.copy
+                    copy(out=cutter[b, j0][:, t, :], in_=bank[:])
 
         def round_weight(copy, name, raw):
             grouped = tile(name, [P, KP * PACK], BF16)
@@ -137,7 +138,7 @@ def tile_list_ground_sensor_larger_kernel(
             return grouped
 
         def round_w3(copy, name, raw):
-            grouped = tile(name, [P, N * PACK], BF16)
+            grouped = tile(name, [P, raw.shape[2] * PACK], BF16)
             copy(
                 out=grouped[:].rearrange("p (c e t) -> p c t e", e=PACK, t=PACK),
                 in_=raw[:].rearrange("p t (c e) -> p c t e", e=PACK),
@@ -166,20 +167,14 @@ def tile_list_ground_sensor_larger_kernel(
         v[1] = gather("v1", tab[1], U32, 0, S)
         w1_bf[0, 1] = tile("w1_bf01", [P, KP * PACK], BF16)
         dealt = w1_bf[0, 1][:].rearrange("p (t u e j) -> p t u j e", t=PACK, e=PACK, j=PACK)
-        source = w1_raw[0, 1][:].rearrange("p j (u t e) -> p t u j e", t=PACK, e=PACK)
-        nc.vector.tensor_copy(out=dealt[:, 0:2], in_=source[:, 0:2])
-        nc.scalar.copy(out=dealt[:, 2:4], in_=source[:, 2:4])
-        w1q[0, 1] = (tile("w1q01_codes", [P, KP], U32), tile("w1q01_scales", [P, KP], U8))
-        for half in range(2):
-            cols = slice(half * KP // 2, (half + 1) * KP // 2)
-            nc.vector.quantize_mx(
-                out=w1q[0, 1][0][:, cols].bitcast(FP8X4),
-                scales=w1q[0, 1][1][:, cols],
-                in_=w1_bf[0, 1][:, half * 2 * KP : (half + 1) * 2 * KP],
-            )
+        source = [raw[:].rearrange("p j (u t e) -> p t u j e", t=PACK, e=PACK) for raw in w1_last]
+        nc.scalar.copy(out=dealt[:, :, 0:16], in_=source[0])
+        nc.vector.tensor_copy(out=dealt[:, 0:2, 16:32], in_=source[1][:, 0:2])
+        nc.scalar.copy(out=dealt[:, 2:4, 16:32], in_=source[1][:, 2:4])
+        w1q[0, 1] = quantize("w1q01", w1_bf[0, 1][:])
         for a in range(2):
             w1_bf[1, a] = round_weight(nc.scalar.copy, f"w1_bf1{a}", w1_raw[1, a])
-        w3_bf = [round_w3(nc.scalar.copy, f"w3_bf{b}", w3_raw[b]) for b in range(2)]
+        w3_bf = [round_w3(nc.scalar.copy, f"w3_bf{b}", w3_raw[b]) for b in range(3)]
 
         banks = {}
 
@@ -208,9 +203,9 @@ def tile_list_ground_sensor_larger_kernel(
             j0 = jc * JC // widths[b] * widths[b]
             c0 = (jc * JC - j0) * PACK
             nc.vector.tensor_tensor(
-                out=h_bf[b, j0][:, c0 : c0 + JC * PACK].rearrange("p (j t) -> p j t", t=PACK),
-                in0=banks[b, jc][:].rearrange("p t j -> p j t"),
-                in1=cutter[b, jc][:],
+                out=h_bf[b, j0][:, c0 : c0 + JC * PACK].rearrange("p (c i t) -> p c t i", i=2, t=PACK),
+                in0=banks[b, jc][:].rearrange("p t (c i) -> p c t i", i=2),
+                in1=cutter[b, jc // 4 * 512][:, :, jc % 4 * JC : (jc % 4 + 1) * JC].rearrange("p t (c i) -> p c t i", i=2),
                 op=ALU.max,
             )
 
@@ -221,34 +216,47 @@ def tile_list_ground_sensor_larger_kernel(
 
         out_v = out.rearrange("(q p) j -> p q j", q=PACK)
 
-        def project(j0, width, per_bank, engines):
-            h0 = (j0 // 512) * 512
-            moving = [
-                (hq[0, h0][0][:, j0 - h0 : j0 - h0 + width], hq[0, h0][1][:, j0 - h0 : j0 - h0 + width]),
-                (hq[1, j0][0][:], hq[1, j0][1][:]),
-            ]
-            for q0 in range(0, PACK, per_bank):
-                bank = psum.tile([P, per_bank, width], F32, name="bank")
+        def y_pass(dst, b, q, j0, start, stop):
+            h0 = j0 // widths[b] * widths[b]
+            cols = slice(j0 - h0, j0 - h0 + YW)
+            n0 = slice(q % 2 * P, (q % 2 + 1) * P)
+            nc.tensor.matmul_mx(
+                out=dst,
+                lhsT=w3q[b, q // 2][0][:, n0].bitcast(FP8X4),
+                lhsT_scale=w3q[b, q // 2][1][:, n0],
+                rhs=hq[b, h0][0][:, cols].bitcast(FP8X4),
+                rhs_scale=hq[b, h0][1][:, cols],
+                start=start,
+                stop=stop,
+            )
+
+        def add_bias_scalar(dst, src, q):
+            nc.scalar.activation(out=dst, in_=src, func=ACT.Identity, bias=bias_sb[:, q : q + 1])
+
+        def add_bias_vector(dst, src, q):
+            nc.vector.tensor_scalar(dst, src, bias_sb[:, q : q + 1], None, ALU.add)
+
+        def project(j0):
+            for q0 in (0, 2):
+                bank = psum.tile([P, 2, YW], F32, name="bank")
                 for b in range(2):
-                    for i in range(per_bank):
-                        q = q0 + i
-                        nc.tensor.matmul_mx(
-                            out=bank[:, i, :],
-                            lhsT=w3q[b][0][:, q * P : (q + 1) * P].bitcast(FP8X4),
-                            lhsT_scale=w3q[b][1][:, q * P : (q + 1) * P],
-                            rhs=moving[b][0].bitcast(FP8X4),
-                            rhs_scale=moving[b][1],
-                            start=(b == 0 and i == 0),
-                            stop=(b == 1 and i == per_bank - 1),
-                        )
-                y = tile(f"y{j0}_{q0}", [P, per_bank, width], F32)
-                for i in range(per_bank):
-                    col = bias_sb[:, q0 + i : q0 + i + 1]
-                    if engines[q0 // per_bank] == "scalar":
-                        nc.scalar.activation(out=y[:, i, :], in_=bank[:, i, :], func=ACT.Identity, bias=col)
-                    else:
-                        nc.vector.tensor_scalar(y[:, i, :], bank[:, i, :], col, None, ALU.add)
-                nc.sync.dma_start(out=out_v[:, q0 : q0 + per_bank, j0 : j0 + width], in_=y[:])
+                    for i in range(2):
+                        y_pass(bank[:, i, :], b, q0 + i, j0, b == 0 and i == 0, b == 1 and i == 1)
+                y = tile(f"y{j0}_{q0}", [P, 2, YW], F32)
+                for i in range(2):
+                    add_bias_scalar(y[:, i, :], bank[:, i, :], q0 + i)
+                nc.sync.dma_start(out=out_v[:, q0 : q0 + 2, j0 : j0 + YW], in_=y[:])
+
+        def project_last(j0):
+            last = [psum.tile([P, YW], F32, name="bank") for q in range(PACK)]
+            for b in range(2):
+                for q in range(PACK):
+                    y_pass(last[q][:], b, q, j0, b == 0, b == 1)
+            for first, add_bias, queue in ((0, add_bias_vector, nc.sync), (1, add_bias_scalar, nc.scalar)):
+                y = tile(f"y{j0}_{first}", [P, 2, YW], F32)
+                for i in range(2):
+                    add_bias(y[:, i, :], last[first + 2 * i][:], first + 2 * i)
+                queue.dma_start(out=out_v[:, first:PACK:2, j0 : j0 + YW], in_=y[:])
 
         w3q = {}
         for jc in range(8):
@@ -264,22 +272,25 @@ def tile_list_ground_sensor_larger_kernel(
             ground(1, jc)
         larger(1, 0)
         h_quant(0, 512)
-        w3q[0] = quantize("w3q0", w3_bf[0][:])
+        codes, scales = quantize("w3q0", w3_bf[0][:])
+        for half in range(2):
+            w3q[0, half] = (codes[:, half * 2 * P : (half + 1) * 2 * P], scales[:, half * 2 * P : (half + 1) * 2 * P])
         larger(1, 1)
-        w3q[1] = quantize("w3q1", w3_bf[1][:])
+        w3q[1, 0] = quantize("w3q10", w3_bf[1][:])
         h_quant(1, 0)
+        w3q[1, 1] = quantize("w3q11", w3_bf[2][:])
         larger(1, 2)
-        project(0, 256, 2, ["scalar", "scalar"])
+        project(0)
         ground(1, 6)
         ground(1, 7)
         larger(1, 3)
         larger(1, 4)
         h_quant(1, 256)
-        project(256, 256, 2, ["scalar", "scalar"])
+        project(256)
         larger(1, 5)
         larger(1, 6)
         h_quant(1, 512)
-        project(512, 256, 2, ["scalar", "scalar"])
+        project(512)
         larger(1, 7)
         h_quant(1, 768)
-        project(768, 256, 2, ["vector", "scalar"])
+        project_last(768)

@@ -19,8 +19,14 @@ ACT = mybir.ActivationFunctionType
 P = 128
 PACK = 4
 KP = P * PACK
-JC = 128
-YW = 256
+QUADRANT = 32
+BANKS = 8
+BANK_W = 512
+UNIT_W = BANK_W // PACK
+UNITS = S // UNIT_W
+OUT_W = 256
+H_W = (512, OUT_W)
+V_PLANE = (4, 8)
 
 
 def tile_list_ground_sensor_larger_kernel(
@@ -29,7 +35,7 @@ def tile_list_ground_sensor_larger_kernel(
     nc = tc.nc
     with ExitStack() as ctx:
         keep = ctx.enter_context(tc.tile_pool(name="keep", bufs=1))
-        psum = ctx.enter_context(tc.psum_pool(name="psum", bufs=8))
+        psum = ctx.enter_context(tc.psum_pool(name="psum", bufs=BANKS))
 
         def tile(name, shape, dtype):
             return keep.tile(shape, dtype, name=name, align_bytes=64)
@@ -41,19 +47,21 @@ def tile_list_ground_sensor_larger_kernel(
         nc.gpsimd.memset(w2_sc_raw[:].bitcast(I32), 0)
         nc.gpsimd.memset(xs_sc[:].bitcast(I32), 0)
         nc.vector.memset(tab_sc[:].bitcast(I32), 0)
+        v_sc = tile("v_sc", [P, S], U8)
+        nc.gpsimd.memset(v_sc[:].bitcast(I32), 0)
 
         w2_raw = tile("w2_raw", [P, 2 * H], U8)
         xs = tile("xs", [P, S], U32)
         nc.sync.dma_start(out=w2_raw[:].bitcast(I32), in_=w2_words[0].bitcast(I32))
         nc.sync.dma_start(out=xs[:].bitcast(I32), in_=xs_words[0].rearrange("p c i -> p (c i)").bitcast(I32))
 
-        def load_scale_row(plane, first, rows, r):
-            nc.sync.dma_start(out=plane[first + r : P : 32, :].bitcast(I32), in_=rows[r:16:4, :].bitcast(I32))
+        def load_scale_rows(plane, rows, live):
+            nc.sync.dma_start(out=plane[live:P:QUADRANT, :].bitcast(I32), in_=rows[live:16:4, :].bitcast(I32))
 
         def load_w1(a, c0, width):
             raw = tile(f"w1_raw{a}_{c0}", [P, PACK, width], F32)
             rows = w1[a * KP : (a + 1) * KP, c0 : c0 + width]
-            nc.sync.dma_start(out=raw[:], in_=rows.rearrange("(p j) c -> p j c", j=PACK))
+            nc.sync.dma_start(out=raw[:], in_=rows.rearrange("(p i) c -> p i c", i=PACK))
             return raw
 
         def load_w3(b, n0, width):
@@ -70,33 +78,28 @@ def tile_list_ground_sensor_larger_kernel(
             words = tab_words[a].rearrange("p t i -> p (t i)").bitcast(I32)
             nc.sync.dma_start(out=tab[a][:, cols].bitcast(I32), in_=words[:, cols])
 
-        def load_tab_scale_row(i):
-            r, a = divmod(i, 2)
-            load_scale_row(tab_sc, 4 + 4 * a, tab_scales[a], r)
+        def gather(name, window, dtype):
+            picked = tile(name, [P, S], dtype)
+            nc.vector.tensor_copy(picked[:], window[:].indirect(offsets[:]))
+            return picked
+
+        def move_scale_rows(a, live):
+            nc.sync.dma_start(
+                out=v_sc[V_PLANE[a] + live : P : QUADRANT, :].bitcast(I32),
+                in_=picked_sc[64 * a + 4 * live : 64 * (a + 1) : 16, :].bitcast(I32),
+            )
 
         w1_raw = {}
-        for r in range(4):
-            load_scale_row(w2_sc_raw, 0, w2_scales[0], r)
-        load_scale_row(xs_sc, 0, xs_scales[0], 0)
-        w1_raw[0, 0] = load_w1(0, 0, KP)
-        for r in range(1, 4):
-            load_scale_row(xs_sc, 0, xs_scales[0], r)
-        load_table(0, 0)
-        for i in range(4):
-            load_tab_scale_row(i)
-        load_table(0, 1)
-        for i in range(4, 8):
-            load_tab_scale_row(i)
+        for live in range(3):
+            load_scale_rows(w2_sc_raw, w2_scales[0], live)
         nc.sync.dma_start(offsets[:], offs)
-        load_table(1, 0)
-        load_table(1, 1)
-        w1_last = [load_w1(1, half * KP // 2, KP // 2) for half in range(2)]
-        w1_raw[1, 0] = load_w1(0, KP, KP)
-        w1_raw[1, 1] = load_w1(1, KP, KP)
-        w3_raw = [load_w3(0, 0, N), load_w3(1, 0, N // 2), load_w3(1, N // 2, N // 2)]
-        bias_sb = tile("bias_sb", [P, PACK], F32)
-        with nc.allow_non_contiguous_dma(reason="one bias value a partition and output tile"):
-            nc.sync.dma_start(out=bias_sb[:], in_=bias.rearrange("(q p) -> p q", q=PACK))
+        nc.sync.dma_start(out=tab_sc[0:P:4, :].bitcast(I32), in_=tab_scales.rearrange("a q t -> (a q) t").bitcast(I32))
+        w1_raw[0, 0] = load_w1(0, 0, KP)
+        load_scale_rows(w2_sc_raw, w2_scales[0], 3)
+        for live in range(4):
+            load_scale_rows(xs_sc, xs_scales[0], live)
+        load_table(0, 0)
+        load_table(0, 1)
 
         w2c = tile("w2c", [P, 2 * H], U8)
         w2s = tile("w2s", [P, H], U8)
@@ -109,14 +112,31 @@ def tile_list_ground_sensor_larger_kernel(
             in_=w2_sc_raw[:].bitcast(I32).rearrange("p (b u t) -> p b t u", b=2, t=PACK),
         )
 
+        picked_sc = gather("picked_sc", tab_sc, U8)
+        moves = [(a, live) for a in range(2) for live in range(4)]
+        first_run = 6
+        for a, live in moves[:first_run]:
+            move_scale_rows(a, live)
+        load_table(1, 0)
+        load_table(1, 1)
+        for a, live in moves[first_run:]:
+            move_scale_rows(a, live)
+        w1_last = [load_w1(1, half * KP // 2, KP // 2) for half in range(2)]
+        w1_raw[1, 0] = load_w1(0, KP, KP)
+        w1_raw[1, 1] = load_w1(1, KP, KP)
+        w3_raw = [load_w3(0, 0, N), load_w3(1, 0, N // 2), load_w3(1, N // 2, N // 2)]
+        bias_sb = tile("bias_sb", [P, PACK], F32)
+        with nc.allow_non_contiguous_dma(reason="one bias value a partition and output tile"):
+            nc.sync.dma_start(out=bias_sb[:], in_=bias.rearrange("(q p) -> p q", q=PACK))
+
         cutter = {}
         for b in range(2):
-            for j0 in range(0, S, 512):
-                cols = slice(j0, j0 + 512)
-                cutter[b, j0] = tile(f"cutter{b}_{j0}", [P, PACK, 512], F32)
+            for j0 in range(0, S, BANK_W):
+                cols = slice(j0, j0 + BANK_W)
+                cutter[b, j0] = tile(f"cutter{b}_{j0}", [P, PACK, BANK_W], F32)
                 for t in range(PACK):
                     c0 = b * KP + t * P
-                    bank = psum.tile([P, 512], F32, name="bank")
+                    bank = psum.tile([P, BANK_W], F32, name="bank")
                     nc.tensor.matmul_mx(
                         out=bank[:],
                         lhsT=w2c[:, 2 * c0 : 2 * (c0 + P)].bitcast(FP4X4),
@@ -129,19 +149,19 @@ def tile_list_ground_sensor_larger_kernel(
                     copy = nc.vector.tensor_copy if b == 0 and t % 2 == 1 else nc.scalar.copy
                     copy(out=cutter[b, j0][:, t, :], in_=bank[:])
 
-        def round_weight(copy, name, raw):
+        def round_w1(copy, name, raw):
             grouped = tile(name, [P, KP * PACK], BF16)
             copy(
-                out=grouped[:].rearrange("p (t u e j) -> p t u j e", t=PACK, e=PACK, j=PACK),
-                in_=raw[:].rearrange("p j (u t e) -> p t u j e", t=PACK, e=PACK),
+                out=grouped[:].rearrange("p (t u e i) -> p t u i e", t=PACK, e=PACK, i=PACK),
+                in_=raw[:].rearrange("p i (u t e) -> p t u i e", t=PACK, e=PACK),
             )
             return grouped
 
-        def round_w3(copy, name, raw):
+        def round_w3(name, raw):
             grouped = tile(name, [P, raw.shape[2] * PACK], BF16)
-            copy(
-                out=grouped[:].rearrange("p (c e t) -> p c t e", e=PACK, t=PACK),
-                in_=raw[:].rearrange("p t (c e) -> p c t e", e=PACK),
+            nc.scalar.copy(
+                out=grouped[:].rearrange("p (c x t) -> p c t x", x=4, t=PACK),
+                in_=raw[:].rearrange("p t (c x) -> p c t x", x=4),
             )
             return grouped
 
@@ -152,80 +172,73 @@ def tile_list_ground_sensor_larger_kernel(
             nc.vector.quantize_mx(out=codes[:].bitcast(FP8X4), scales=scales[:], in_=grouped)
             return codes, scales
 
-        def gather(name, window, dtype, j0, width):
-            picked = tile(name, [P, width], dtype)
-            nc.vector.tensor_copy(picked[:], window[:].indirect(offsets[:, j0 // 16 : (j0 + width) // 16]))
-            return picked
-
         w1q = {}
         w1_bf = {}
-        w1_bf[0, 0] = round_weight(nc.vector.tensor_copy, "w1_bf00", w1_raw[0, 0])
-        v_sc = gather("v_sc", tab_sc, U8, 0, S)
+        w1_bf[0, 0] = round_w1(nc.vector.tensor_copy, "w1_bf00", w1_raw[0, 0])
         w1q[0, 0] = quantize("w1q00", w1_bf[0, 0][:])
-        v = {}
-        v[0] = gather("v0", tab[0], U32, 0, S)
-        v[1] = gather("v1", tab[1], U32, 0, S)
+        v = [gather(f"v{a}", tab[a], U32) for a in range(2)]
         w1_bf[0, 1] = tile("w1_bf01", [P, KP * PACK], BF16)
-        dealt = w1_bf[0, 1][:].rearrange("p (t u e j) -> p t u j e", t=PACK, e=PACK, j=PACK)
-        source = [raw[:].rearrange("p j (u t e) -> p t u j e", t=PACK, e=PACK) for raw in w1_last]
+        dealt = w1_bf[0, 1][:].rearrange("p (t u e i) -> p t u i e", t=PACK, e=PACK, i=PACK)
+        source = [raw[:].rearrange("p i (u t e) -> p t u i e", t=PACK, e=PACK) for raw in w1_last]
         nc.scalar.copy(out=dealt[:, :, 0:16], in_=source[0])
         nc.vector.tensor_copy(out=dealt[:, 0:2, 16:32], in_=source[1][:, 0:2])
         nc.scalar.copy(out=dealt[:, 2:4, 16:32], in_=source[1][:, 2:4])
         w1q[0, 1] = quantize("w1q01", w1_bf[0, 1][:])
         for a in range(2):
-            w1_bf[1, a] = round_weight(nc.scalar.copy, f"w1_bf1{a}", w1_raw[1, a])
-        w3_bf = [round_w3(nc.scalar.copy, f"w3_bf{b}", w3_raw[b]) for b in range(3)]
+            w1_bf[1, a] = round_w1(nc.scalar.copy, f"w1_bf1{a}", w1_raw[1, a])
+        w3_bf = [round_w3(f"w3_bf{piece}", raw) for piece, raw in enumerate(w3_raw)]
 
         banks = {}
 
-        def ground(b, jc):
-            cols = slice(jc * JC, (jc + 1) * JC)
-            banks[b, jc] = psum.tile([P, PACK, JC], F32, name="bank")
+        def ground(b, unit):
+            cols = slice(unit * UNIT_W, (unit + 1) * UNIT_W)
+            banks[b, unit] = psum.tile([P, PACK, UNIT_W], F32, name="bank")
             for a in range(2):
                 codes, scales = w1q[b, a]
                 for t in range(PACK):
                     nc.tensor.matmul_mx(
-                        out=banks[b, jc][:, t, :],
+                        out=banks[b, unit][:, t, :],
                         lhsT=codes[:, t * P : (t + 1) * P].bitcast(FP8X4),
                         lhsT_scale=scales[:, t * P : (t + 1) * P],
                         rhs=v[a][:, cols].bitcast(FP8X4),
-                        rhs_scale=v_sc[4 + 4 * a : P, cols],
+                        rhs_scale=v_sc[V_PLANE[a] : P, cols],
                         start=(a == 0 and t == 0),
                         stop=(a == 1 and t == PACK - 1),
                     )
 
-        widths = (512, 256)
-        h_bf = {
-            (b, j0): tile(f"h_bf{b}_{j0}", [P, widths[b] * PACK], BF16) for b in range(2) for j0 in range(0, S, widths[b])
-        }
+        h_bf = {(b, j0): tile(f"h_bf{b}_{j0}", [P, H_W[b] * PACK], BF16) for b in range(2) for j0 in range(0, S, H_W[b])}
 
-        def larger(b, jc):
-            j0 = jc * JC // widths[b] * widths[b]
-            c0 = (jc * JC - j0) * PACK
+        def larger(b, unit):
+            j = unit * UNIT_W
+            in_h = j % H_W[b]
+            in_cutter = j % BANK_W
             nc.vector.tensor_tensor(
-                out=h_bf[b, j0][:, c0 : c0 + JC * PACK].rearrange("p (c i t) -> p c t i", i=2, t=PACK),
-                in0=banks[b, jc][:].rearrange("p t (c i) -> p c t i", i=2),
-                in1=cutter[b, jc // 4 * 512][:, :, jc % 4 * JC : (jc % 4 + 1) * JC].rearrange("p t (c i) -> p c t i", i=2),
+                out=h_bf[b, j - in_h][:, in_h * PACK : (in_h + UNIT_W) * PACK].rearrange(
+                    "p (c x t) -> p c t x", x=2, t=PACK
+                ),
+                in0=banks[b, unit][:].rearrange("p t (c x) -> p c t x", x=2),
+                in1=cutter[b, j - in_cutter][:, :, in_cutter : in_cutter + UNIT_W].rearrange("p t (c x) -> p c t x", x=2),
                 op=ALU.max,
             )
 
         hq = {}
 
-        def h_quant(b, j0):
+        def quantize_h(b, j0):
             hq[b, j0] = quantize(f"hq{b}_{j0}", h_bf[b, j0][:])
 
         out_v = out.rearrange("(q p) j -> p q j", q=PACK)
+        w3q = {}
 
-        def y_pass(dst, b, q, j0, start, stop):
-            h0 = j0 // widths[b] * widths[b]
-            cols = slice(j0 - h0, j0 - h0 + YW)
-            n0 = slice(q % 2 * P, (q % 2 + 1) * P)
+        def out_pass(dst, b, q, j0, start, stop):
+            in_h = j0 % H_W[b]
+            cols = slice(in_h, in_h + OUT_W)
+            rows = slice(q % 2 * P, (q % 2 + 1) * P)
             nc.tensor.matmul_mx(
                 out=dst,
-                lhsT=w3q[b, q // 2][0][:, n0].bitcast(FP8X4),
-                lhsT_scale=w3q[b, q // 2][1][:, n0],
-                rhs=hq[b, h0][0][:, cols].bitcast(FP8X4),
-                rhs_scale=hq[b, h0][1][:, cols],
+                lhsT=w3q[b, q // 2][0][:, rows].bitcast(FP8X4),
+                lhsT_scale=w3q[b, q // 2][1][:, rows],
+                rhs=hq[b, j0 - in_h][0][:, cols].bitcast(FP8X4),
+                rhs_scale=hq[b, j0 - in_h][1][:, cols],
                 start=start,
                 stop=stop,
             )
@@ -238,59 +251,60 @@ def tile_list_ground_sensor_larger_kernel(
 
         def project(j0):
             for q0 in (0, 2):
-                bank = psum.tile([P, 2, YW], F32, name="bank")
+                bank = psum.tile([P, 2, OUT_W], F32, name="bank")
                 for b in range(2):
-                    for i in range(2):
-                        y_pass(bank[:, i, :], b, q0 + i, j0, b == 0 and i == 0, b == 1 and i == 1)
-                y = tile(f"y{j0}_{q0}", [P, 2, YW], F32)
-                for i in range(2):
-                    add_bias_scalar(y[:, i, :], bank[:, i, :], q0 + i)
-                nc.sync.dma_start(out=out_v[:, q0 : q0 + 2, j0 : j0 + YW], in_=y[:])
+                    for side in range(2):
+                        out_pass(bank[:, side, :], b, q0 + side, j0, b == 0 and side == 0, b == 1 and side == 1)
+                y = tile(f"y{j0}_{q0}", [P, 2, OUT_W], F32)
+                for side in range(2):
+                    add_bias_scalar(y[:, side, :], bank[:, side, :], q0 + side)
+                nc.sync.dma_start(out=out_v[:, q0 : q0 + 2, j0 : j0 + OUT_W], in_=y[:])
 
         def project_last(j0):
-            last = [psum.tile([P, YW], F32, name="bank") for q in range(PACK)]
+            last = [psum.tile([P, OUT_W], F32, name="bank") for q in range(PACK)]
             for b in range(2):
                 for q in range(PACK):
-                    y_pass(last[q][:], b, q, j0, b == 0, b == 1)
+                    out_pass(last[q][:], b, q, j0, b == 0, b == 1)
             for first, add_bias, queue in ((0, add_bias_vector, nc.sync), (1, add_bias_scalar, nc.scalar)):
-                y = tile(f"y{j0}_{first}", [P, 2, YW], F32)
-                for i in range(2):
-                    add_bias(y[:, i, :], last[first + 2 * i][:], first + 2 * i)
-                queue.dma_start(out=out_v[:, first:PACK:2, j0 : j0 + YW], in_=y[:])
+                y = tile(f"y{j0}_{first}", [P, 2, OUT_W], F32)
+                for side in range(2):
+                    add_bias(y[:, side, :], last[first + 2 * side][:], first + 2 * side)
+                queue.dma_start(out=out_v[:, first:PACK:2, j0 : j0 + OUT_W], in_=y[:])
 
-        w3q = {}
-        for jc in range(8):
-            ground(0, jc)
-            larger(0, jc)
-            if jc == 3:
+        after_w1q, after_hq = 4, 5
+        for unit in range(UNITS):
+            ground(0, unit)
+            larger(0, unit)
+            if unit == after_w1q:
                 w1q[1, 0] = quantize("w1q10", w1_bf[1, 0][:])
-            if jc == 4:
-                h_quant(0, 0)
-            if jc == 5:
-                w1q[1, 1] = quantize("w1q11", w1_bf[1, 1][:])
-        for jc in range(6):
-            ground(1, jc)
+            if unit == after_hq:
+                quantize_h(0, 0)
+        w1q[1, 1] = quantize("w1q11", w1_bf[1, 1][:])
+
+        ahead = BANKS - 2
+        for unit in range(ahead):
+            ground(1, unit)
+        quantize_h(0, H_W[0])
         larger(1, 0)
-        h_quant(0, 512)
+        larger(1, 1)
         codes, scales = quantize("w3q0", w3_bf[0][:])
         for half in range(2):
             w3q[0, half] = (codes[:, half * 2 * P : (half + 1) * 2 * P], scales[:, half * 2 * P : (half + 1) * 2 * P])
-        larger(1, 1)
-        w3q[1, 0] = quantize("w3q10", w3_bf[1][:])
-        h_quant(1, 0)
-        w3q[1, 1] = quantize("w3q11", w3_bf[2][:])
         larger(1, 2)
-        project(0)
-        ground(1, 6)
-        ground(1, 7)
+        quantize_h(1, 0)
+        w3q[1, 0] = quantize("w3q10", w3_bf[1][:])
         larger(1, 3)
+        w3q[1, 1] = quantize("w3q11", w3_bf[2][:])
+        project(0)
+        for unit in range(ahead, UNITS):
+            ground(1, unit)
         larger(1, 4)
-        h_quant(1, 256)
-        project(256)
+        quantize_h(1, OUT_W)
+        project(OUT_W)
         larger(1, 5)
         larger(1, 6)
-        h_quant(1, 512)
-        project(512)
+        quantize_h(1, 2 * OUT_W)
+        project(2 * OUT_W)
         larger(1, 7)
-        h_quant(1, 768)
-        project_last(768)
+        quantize_h(1, 3 * OUT_W)
+        project_last(3 * OUT_W)

from contextlib import ExitStack

import concourse.mybir as mybir

K, T, S, K2, H, N = 1024, 4096, 1024, 512, 1024, 512
FLOPS = 2 * S * (K * H + K2 * H + H * N)

F32 = mybir.dt.float32
BF16 = mybir.dt.bfloat16
I32 = mybir.dt.int32
U32 = mybir.dt.uint32
U16 = mybir.dt.uint16
U8 = mybir.dt.uint8
FP8X4 = mybir.dt.float8_e4m3fn_x4
FP4X4 = mybir.dt.float4_e2m1fn_x4
ALU = mybir.AluOpType
ACT = mybir.ActivationFunctionType

P = 128
PACK = 4
KP = P * PACK
QUADRANT = 32
BANKS = 8
BANK_W = 512
UNIT_W = BANK_W // PACK
UNITS = S // UNIT_W
OUT_W = 256
H_W = (512, OUT_W)
V_PLANE = (4, 8)


def tile_list_ground_sensor_larger_kernel(
    tc, tab_words, tab_scales, offs, xs_words, xs_scales, w1, w2_words, w2_scales, w3, bias, out
):
    nc = tc.nc
    with ExitStack() as ctx:
        keep = ctx.enter_context(tc.tile_pool(name="keep", bufs=1))
        psum = ctx.enter_context(tc.psum_pool(name="psum", bufs=BANKS))

        def tile(name, shape, dtype):
            return keep.tile(shape, dtype, name=name, align_bytes=64)

        offsets = keep.tile([P, S // 16], U16, name="offsets")
        w2_sc_raw = tile("w2_sc_raw", [P, H], U8)
        xs_sc = tile("xs_sc", [P, S], U8)
        tab_sc = tile("tab_sc", [P, T], U8)
        nc.gpsimd.memset(w2_sc_raw[:].bitcast(I32), 0)
        nc.gpsimd.memset(xs_sc[:].bitcast(I32), 0)
        nc.vector.memset(tab_sc[:].bitcast(I32), 0)
        v_sc = tile("v_sc", [P, S], U8)
        nc.gpsimd.memset(v_sc[:].bitcast(I32), 0)

        w2_raw = tile("w2_raw", [P, 2 * H], U8)
        xs = tile("xs", [P, S], U32)
        nc.sync.dma_start(out=w2_raw[:].bitcast(I32), in_=w2_words[0].bitcast(I32))
        nc.sync.dma_start(out=xs[:].bitcast(I32), in_=xs_words[0].rearrange("p c i -> p (c i)").bitcast(I32))

        def load_scale_rows(plane, rows, live):
            nc.sync.dma_start(out=plane[live:P:QUADRANT, :].bitcast(I32), in_=rows[live:16:4, :].bitcast(I32))

        def load_w1(a, c0, width):
            raw = tile(f"w1_raw{a}_{c0}", [P, PACK, width], F32)
            rows = w1[a * KP : (a + 1) * KP, c0 : c0 + width]
            nc.sync.dma_start(out=raw[:], in_=rows.rearrange("(p i) c -> p i c", i=PACK))
            return raw

        def load_w3(b, n0, width):
            raw = tile(f"w3_raw{b}_{n0}", [P, PACK, width], F32)
            rows = w3[b * KP : (b + 1) * KP, n0 : n0 + width].rearrange("(u t e) n -> t u e n", t=PACK, e=PACK)
            for t in range(PACK):
                nc.sync.dma_start(out=raw[:, t, :], in_=rows[t])
            return raw

        tab = [tile(f"tab{a}", [P, T], U32) for a in range(2)]

        def load_table(a, half):
            cols = slice(half * T // 2, (half + 1) * T // 2)
            words = tab_words[a].rearrange("p t i -> p (t i)").bitcast(I32)
            nc.sync.dma_start(out=tab[a][:, cols].bitcast(I32), in_=words[:, cols])

        def gather(name, window, dtype):
            picked = tile(name, [P, S], dtype)
            nc.vector.tensor_copy(picked[:], window[:].indirect(offsets[:]))
            return picked

        def move_scale_rows(a, live):
            nc.sync.dma_start(
                out=v_sc[V_PLANE[a] + live : P : QUADRANT, :].bitcast(I32),
                in_=picked_sc[64 * a + 4 * live : 64 * (a + 1) : 16, :].bitcast(I32),
            )

        w1_raw = {}
        for live in range(3):
            load_scale_rows(w2_sc_raw, w2_scales[0], live)
        nc.sync.dma_start(offsets[:], offs)
        nc.sync.dma_start(out=tab_sc[0:P:4, :].bitcast(I32), in_=tab_scales.rearrange("a q t -> (a q) t").bitcast(I32))
        w1_raw[0, 0] = load_w1(0, 0, KP)
        load_scale_rows(w2_sc_raw, w2_scales[0], 3)
        for live in range(4):
            load_scale_rows(xs_sc, xs_scales[0], live)
        load_table(0, 0)
        load_table(0, 1)

        w2c = tile("w2c", [P, 2 * H], U8)
        w2s = tile("w2s", [P, H], U8)
        nc.vector.tensor_copy(
            out=w2c[:].bitcast(I32).rearrange("p (b t u w) -> p b t u w", b=2, t=PACK, w=2),
            in_=w2_raw[:].bitcast(I32).rearrange("p (b u t w) -> p b t u w", b=2, t=PACK, w=2),
        )
        nc.vector.tensor_copy(
            out=w2s[:].bitcast(I32).rearrange("p (b t u) -> p b t u", b=2, t=PACK),
            in_=w2_sc_raw[:].bitcast(I32).rearrange("p (b u t) -> p b t u", b=2, t=PACK),
        )

        picked_sc = gather("picked_sc", tab_sc, U8)
        moves = [(a, live) for a in range(2) for live in range(4)]
        first_run = 6
        for a, live in moves[:first_run]:
            move_scale_rows(a, live)
        load_table(1, 0)
        load_table(1, 1)
        for a, live in moves[first_run:]:
            move_scale_rows(a, live)
        w1_last = [load_w1(1, half * KP // 2, KP // 2) for half in range(2)]
        w1_raw[1, 0] = load_w1(0, KP, KP)
        w1_raw[1, 1] = load_w1(1, KP, KP)
        w3_raw = [load_w3(0, 0, N), load_w3(1, 0, N // 2), load_w3(1, N // 2, N // 2)]
        bias_sb = tile("bias_sb", [P, PACK], F32)
        with nc.allow_non_contiguous_dma(reason="one bias value a partition and output tile"):
            nc.sync.dma_start(out=bias_sb[:], in_=bias.rearrange("(q p) -> p q", q=PACK))

        cutter = {}
        for b in range(2):
            for j0 in range(0, S, BANK_W):
                cols = slice(j0, j0 + BANK_W)
                cutter[b, j0] = tile(f"cutter{b}_{j0}", [P, PACK, BANK_W], F32)
                for t in range(PACK):
                    c0 = b * KP + t * P
                    bank = psum.tile([P, BANK_W], F32, name="bank")
                    nc.tensor.matmul_mx(
                        out=bank[:],
                        lhsT=w2c[:, 2 * c0 : 2 * (c0 + P)].bitcast(FP4X4),
                        lhsT_scale=w2s[:, c0 : c0 + P],
                        rhs=xs[:, cols].bitcast(FP8X4),
                        rhs_scale=xs_sc[:, cols],
                        start=True,
                        stop=True,
                    )
                    copy = nc.vector.tensor_copy if b == 0 and t % 2 == 1 else nc.scalar.copy
                    copy(out=cutter[b, j0][:, t, :], in_=bank[:])

        def round_w1(copy, name, raw):
            grouped = tile(name, [P, KP * PACK], BF16)
            copy(
                out=grouped[:].rearrange("p (t u e i) -> p t u i e", t=PACK, e=PACK, i=PACK),
                in_=raw[:].rearrange("p i (u t e) -> p t u i e", t=PACK, e=PACK),
            )
            return grouped

        def round_w3(name, raw):
            grouped = tile(name, [P, raw.shape[2] * PACK], BF16)
            nc.scalar.copy(
                out=grouped[:].rearrange("p (c x t) -> p c t x", x=4, t=PACK),
                in_=raw[:].rearrange("p t (c x) -> p c t x", x=4),
            )
            return grouped

        def quantize(name, grouped):
            width = grouped.shape[1] // PACK
            codes = tile(name + "_codes", [P, width], U32)
            scales = tile(name + "_scales", [P, width], U8)
            nc.vector.quantize_mx(out=codes[:].bitcast(FP8X4), scales=scales[:], in_=grouped)
            return codes, scales

        w1q = {}
        w1_bf = {}
        w1_bf[0, 0] = round_w1(nc.vector.tensor_copy, "w1_bf00", w1_raw[0, 0])
        w1q[0, 0] = quantize("w1q00", w1_bf[0, 0][:])
        v = [gather(f"v{a}", tab[a], U32) for a in range(2)]
        w1_bf[0, 1] = tile("w1_bf01", [P, KP * PACK], BF16)
        dealt = w1_bf[0, 1][:].rearrange("p (t u e i) -> p t u i e", t=PACK, e=PACK, i=PACK)
        source = [raw[:].rearrange("p i (u t e) -> p t u i e", t=PACK, e=PACK) for raw in w1_last]
        nc.scalar.copy(out=dealt[:, :, 0:16], in_=source[0])
        nc.vector.tensor_copy(out=dealt[:, 0:2, 16:32], in_=source[1][:, 0:2])
        nc.scalar.copy(out=dealt[:, 2:4, 16:32], in_=source[1][:, 2:4])
        w1q[0, 1] = quantize("w1q01", w1_bf[0, 1][:])
        for a in range(2):
            w1_bf[1, a] = round_w1(nc.scalar.copy, f"w1_bf1{a}", w1_raw[1, a])
        w3_bf = [round_w3(f"w3_bf{piece}", raw) for piece, raw in enumerate(w3_raw)]

        banks = {}

        def ground(b, unit):
            cols = slice(unit * UNIT_W, (unit + 1) * UNIT_W)
            banks[b, unit] = psum.tile([P, PACK, UNIT_W], F32, name="bank")
            for a in range(2):
                codes, scales = w1q[b, a]
                for t in range(PACK):
                    nc.tensor.matmul_mx(
                        out=banks[b, unit][:, t, :],
                        lhsT=codes[:, t * P : (t + 1) * P].bitcast(FP8X4),
                        lhsT_scale=scales[:, t * P : (t + 1) * P],
                        rhs=v[a][:, cols].bitcast(FP8X4),
                        rhs_scale=v_sc[V_PLANE[a] : P, cols],
                        start=(a == 0 and t == 0),
                        stop=(a == 1 and t == PACK - 1),
                    )

        h_bf = {(b, j0): tile(f"h_bf{b}_{j0}", [P, H_W[b] * PACK], BF16) for b in range(2) for j0 in range(0, S, H_W[b])}

        def larger(b, unit):
            j = unit * UNIT_W
            in_h = j % H_W[b]
            in_cutter = j % BANK_W
            nc.vector.tensor_tensor(
                out=h_bf[b, j - in_h][:, in_h * PACK : (in_h + UNIT_W) * PACK].rearrange(
                    "p (c x t) -> p c t x", x=2, t=PACK
                ),
                in0=banks[b, unit][:].rearrange("p t (c x) -> p c t x", x=2),
                in1=cutter[b, j - in_cutter][:, :, in_cutter : in_cutter + UNIT_W].rearrange("p t (c x) -> p c t x", x=2),
                op=ALU.max,
            )

        hq = {}

        def quantize_h(b, j0):
            hq[b, j0] = quantize(f"hq{b}_{j0}", h_bf[b, j0][:])

        out_v = out.rearrange("(q p) j -> p q j", q=PACK)
        w3q = {}

        def out_pass(dst, b, q, j0, start, stop):
            in_h = j0 % H_W[b]
            cols = slice(in_h, in_h + OUT_W)
            rows = slice(q % 2 * P, (q % 2 + 1) * P)
            nc.tensor.matmul_mx(
                out=dst,
                lhsT=w3q[b, q // 2][0][:, rows].bitcast(FP8X4),
                lhsT_scale=w3q[b, q // 2][1][:, rows],
                rhs=hq[b, j0 - in_h][0][:, cols].bitcast(FP8X4),
                rhs_scale=hq[b, j0 - in_h][1][:, cols],
                start=start,
                stop=stop,
            )

        def add_bias_scalar(dst, src, q):
            nc.scalar.activation(out=dst, in_=src, func=ACT.Identity, bias=bias_sb[:, q : q + 1])

        def add_bias_vector(dst, src, q):
            nc.vector.tensor_scalar(dst, src, bias_sb[:, q : q + 1], None, ALU.add)

        def project(j0):
            for q0 in (0, 2):
                bank = psum.tile([P, 2, OUT_W], F32, name="bank")
                for b in range(2):
                    for side in range(2):
                        out_pass(bank[:, side, :], b, q0 + side, j0, b == 0 and side == 0, b == 1 and side == 1)
                y = tile(f"y{j0}_{q0}", [P, 2, OUT_W], F32)
                for side in range(2):
                    add_bias_scalar(y[:, side, :], bank[:, side, :], q0 + side)
                nc.sync.dma_start(out=out_v[:, q0 : q0 + 2, j0 : j0 + OUT_W], in_=y[:])

        def project_last(j0):
            last = [psum.tile([P, OUT_W], F32, name="bank") for q in range(PACK)]
            for b in range(2):
                for q in range(PACK):
                    out_pass(last[q][:], b, q, j0, b == 0, b == 1)
            for first, add_bias, queue in ((0, add_bias_vector, nc.sync), (1, add_bias_scalar, nc.scalar)):
                y = tile(f"y{j0}_{first}", [P, 2, OUT_W], F32)
                for side in range(2):
                    add_bias(y[:, side, :], last[first + 2 * side][:], first + 2 * side)
                queue.dma_start(out=out_v[:, first:PACK:2, j0 : j0 + OUT_W], in_=y[:])

        after_w1q, after_hq = 4, 5
        for unit in range(UNITS):
            ground(0, unit)
            larger(0, unit)
            if unit == after_w1q:
                w1q[1, 0] = quantize("w1q10", w1_bf[1, 0][:])
            if unit == after_hq:
                quantize_h(0, 0)
        w1q[1, 1] = quantize("w1q11", w1_bf[1, 1][:])

        ahead = BANKS - 2
        for unit in range(ahead):
            ground(1, unit)
        quantize_h(0, H_W[0])
        larger(1, 0)
        larger(1, 1)
        codes, scales = quantize("w3q0", w3_bf[0][:])
        for half in range(2):
            w3q[0, half] = (codes[:, half * 2 * P : (half + 1) * 2 * P], scales[:, half * 2 * P : (half + 1) * 2 * P])
        larger(1, 2)
        quantize_h(1, 0)
        w3q[1, 0] = quantize("w3q10", w3_bf[1][:])
        larger(1, 3)
        w3q[1, 1] = quantize("w3q11", w3_bf[2][:])
        project(0)
        for unit in range(ahead, UNITS):
            ground(1, unit)
        larger(1, 4)
        quantize_h(1, OUT_W)
        project(OUT_W)
        larger(1, 5)
        larger(1, 6)
        quantize_h(1, 2 * OUT_W)
        project(2 * OUT_W)
        larger(1, 7)
        quantize_h(1, 3 * OUT_W)
        project_last(3 * OUT_W)
